import numpy as np
import ml_dtypes


def mxq(x, axis, fmt="e4m3"):
    dtype, down = {"e4m3": (ml_dtypes.float8_e4m3fn, 7), "e5m2": (ml_dtypes.float8_e5m2, 14)}[fmt]
    v = np.moveaxis(np.asarray(x, np.float32).astype(ml_dtypes.bfloat16).astype(np.float64), axis, -1)
    blocks = v.reshape(v.shape[:-1] + (-1, 32))
    amax = np.abs(blocks).max(-1, keepdims=True)
    byte = np.maximum(np.where(amax > 0, np.frexp(amax)[1] - 1 + 127, 0) - down, 1)
    scale = np.exp2(byte - 127.0)
    codes = (blocks / scale).astype(np.float32).astype(dtype).astype(np.float64)
    return np.moveaxis((codes * scale).reshape(v.shape), -1, axis)


WIDE = False


def mx_kscale(k, group=512):
    if not WIDE:
        return np.ones(k)
    levels = np.array([18, -18])
    if group != 512:
        return np.exp2(np.random.permutation(np.resize(levels, k // group))).repeat(group)
    if k % 512:
        return np.exp2(np.random.permutation(np.resize(levels, k // 32))).repeat(32)
    a = np.empty((k // 512, 16))
    for p in range(k // 512):
        a[p, :8] = np.random.permutation(np.resize(levels, 8))
        for g in range(8):
            far = levels[np.abs(levels - a[p, g]) >= 10]
            a[p, g + 8] = far[np.random.randint(len(far))]
    return np.exp2(a.ravel()).repeat(32)


def f64(x):
    return np.asarray(x).astype(np.float64)


G, D, M, N = 8, 128, 128, 512


def setup_inputs():
    n = np.random.standard_normal
    s = mx_kscale(D, 0)[:, None]
    return {
        "x": (n((G, D, N)) * s).astype(np.float32),
        "w": (n((G, D, M)) / np.sqrt(D) / s).astype(np.float32),
        "u": (n((G, D, M)) / np.sqrt(D) / s).astype(np.float32),
        "b": (0.5 * n((G, M, 1))).astype(np.float32),
    }


def reference(x, w, u, b):
    xq = mxq(f64(x), 1, "e4m3")
    h = mxq(f64(w), 1, "e4m3").transpose(0, 2, 1) @ xq
    g = mxq(f64(u), 1, "e4m3").transpose(0, 2, 1) @ xq
    h = h + f64(b)
    y = np.tanh(h) * g
    return y

@@ -1,0 +1,187 @@
+from contextlib import ExitStack
+
+import concourse.mybir as mybir
+
+G, D, M, N = 8, 128, 128, 512
+FLOPS = 2 * 2 * G * D * M * N
+
+F32 = mybir.dt.float32
+BF16 = mybir.dt.bfloat16
+U32 = mybir.dt.uint32
+U8 = mybir.dt.uint8
+FP8X4 = mybir.dt.float8_e4m3fn_x4
+ACT = mybir.ActivationFunctionType
+ALU = mybir.AluOpType
+
+P = 128
+PACK = 4
+ROWS = 32
+SIDE = 4
+SETS = G // SIDE
+NMM = 128
+W = 256
+RUN = 4
+
+
+def interleave(copy, dst, src, lo, hi):
+    copy(
+        out=dst[:, lo:hi, :].rearrange("p (c i) t -> p c t i", i=RUN),
+        in_=src[:, :, lo:hi].rearrange("p t (c i) -> p c t i", i=RUN),
+    )
+
+
+def tile_rows_gglu_tanh_bias_kernel(tc, x, w, u, b, out):
+    nc = tc.nc
+    x_rows = x.rearrange("g d n -> (g d) n")
+    w_rows = w.rearrange("g d m -> (g d) m")
+    u_rows = u.rearrange("g d m -> (g d) m")
+    b_rows = b.rearrange("g m o -> g (m o)")
+    chunks = [(s, n0) for s in range(SETS) for n0 in range(0, N, W)]
+
+    def set_rows(rows, s):
+        return rows[s * P * PACK : (s + 1) * P * PACK, :].rearrange("(p j) n -> p j n", j=PACK)
+
+    with ExitStack() as ctx:
+        sb = ctx.enter_context(tc.tile_pool(name="sb", bufs=1))
+        ps = ctx.enter_context(tc.psum_pool(name="ps", bufs=1))
+        ctx.enter_context(tc.manual_schedule())
+
+        def tiles(name, count, shape, dtype):
+            return [sb.tile(shape, dtype, name="%s%d" % (name, i), align_bytes=64) for i in range(count)]
+
+        w_raw = tiles("w_raw", SETS, [P, PACK, M], F32)
+        u_raw = tiles("u_raw", SETS, [P, PACK, M], F32)
+        w_bf = tiles("w_bf", SETS, [P, M, PACK], BF16)
+        u_bf = tiles("u_bf", SETS, [P, M, PACK], BF16)
+        w_codes = tiles("w_codes", SETS, [P, M], U32)
+        u_codes = tiles("u_codes", SETS, [P, M], U32)
+        w_scales = tiles("w_scales", SETS, [P, M], U8)
+        u_scales = tiles("u_scales", SETS, [P, M], U8)
+        x_raw = tiles("x_raw", len(chunks), [P, PACK, W], F32)
+        x_bf = tiles("x_bf", len(chunks), [P, W, PACK], BF16)
+        x_codes = tiles("x_codes", len(chunks), [P, W], U32)
+        x_scales = tiles("x_scales", len(chunks), [P, W], U8)
+        act = tiles("act", G, [P, N], F32)
+        y = tiles("y", SETS, [P, SIDE, N], F32)
+        b_stage = sb.tile([P, ROWS], F32, name="b_stage", align_bytes=64)
+        b_cols = sb.tile([P, ROWS], F32, name="b_cols", align_bytes=64)
+        h_bank = [ps.tile([P, N], F32, name="h_bank%d" % c) for c in range(SIDE)]
+        g_bank = [ps.tile([P, N], F32, name="g_bank%d" % c) for c in range(SIDE)]
+
+        def load_x(k):
+            s, n0 = chunks[k]
+            nc.sync.dma_start(out=x_raw[k][:], in_=set_rows(x_rows, s)[:, :, n0 : n0 + W])
+
+        def load_wu(s):
+            nc.sync.dma_start(out=w_raw[s][:], in_=set_rows(w_rows, s))
+            nc.sync.dma_start(out=u_raw[s][:], in_=set_rows(u_rows, s))
+
+        def quantize(codes, scales, bf):
+            nc.vector.quantize_mx(
+                out=codes[:].bitcast(FP8X4), scales=scales[:], in_=bf[:].rearrange("p n t -> p (n t)")
+            )
+
+        def v_il(dst, src, lo, hi):
+            interleave(nc.vector.tensor_copy, dst, src, lo, hi)
+
+        def s_il(dst, src, lo, hi):
+            interleave(nc.scalar.copy, dst, src, lo, hi)
+
+        def products(k):
+            s, n0 = chunks[k]
+            for banks, codes, scales in ((h_bank, w_codes, w_scales), (g_bank, u_codes, u_scales)):
+                for o in range(0, W, NMM):
+                    for c in range(SIDE):
+                        r = slice(ROWS * c, ROWS * (c + 1))
+                        nc.tensor.matmul_mx(
+                            out=banks[c][:, n0 + o : n0 + o + NMM],
+                            lhsT=codes[s][r, :].bitcast(FP8X4),
+                            lhsT_scale=scales[s][r, :],
+                            rhs=x_codes[k][r, o : o + NMM].bitcast(FP8X4),
+                            rhs_scale=x_scales[k][r, o : o + NMM],
+                            start=True,
+                            stop=True,
+                        )
+
+        def tanh(k, c):
+            s, n0 = chunks[k]
+            g = SIDE * s + c
+            nc.scalar.activation(
+                out=act[g][:, n0 : n0 + W], in_=h_bank[c][:, n0 : n0 + W], func=ACT.Tanh, bias=b_cols[:, g : g + 1]
+            )
+
+        def gate(k, c):
+            s, n0 = chunks[k]
+            g = SIDE * s + c
+            nc.vector.tensor_tensor(
+                out=y[s][:, c, n0 : n0 + W], in0=g_bank[c][:, n0 : n0 + W], in1=act[g][:, n0 : n0 + W], op=ALU.mult
+            )
+
+        def store(s, c0, c1, n0, n1):
+            g0 = SIDE * s
+            nc.sync.dma_start(
+                out=out[g0 + c0 : g0 + c1, :, n0:n1].rearrange("g m n -> m g n"), in_=y[s][:, c0:c1, n0:n1]
+            )
+
+        load_wu(0)
+        load_x(0)
+        load_x(1)
+        load_wu(1)
+        load_x(2)
+        load_x(3)
+        nc.gpsimd.memset(b_stage[:], 0.0)
+        for q in range(SIDE):
+            nc.gpsimd.dma_start(out=b_stage[ROWS * q : ROWS * q + G, :], in_=b_rows[:, ROWS * q : ROWS * (q + 1)])
+
+        v_il(w_bf[0], w_raw[0], 0, M)
+        v_il(u_bf[0], u_raw[0], 0, M)
+        quantize(w_codes[0], w_scales[0], w_bf[0])
+        quantize(u_codes[0], u_scales[0], u_bf[0])
+        v_il(x_bf[0], x_raw[0], 0, W)
+        nc.vector.transpose(out=b_cols[:], in_=b_stage[:])
+        quantize(x_codes[0], x_scales[0], x_bf[0])
+        products(0)
+        v_il(x_bf[1], x_raw[1], 0, W)
+        for c in range(SIDE):
+            tanh(0, c)
+        gate(0, 0)
+        quantize(x_codes[1], x_scales[1], x_bf[1])
+        products(1)
+        s_il(w_bf[1], w_raw[1], 0, M)
+        gate(0, 1)
+        gate(0, 2)
+        gate(0, 3)
+        v_il(u_bf[1], u_raw[1], 0, M)
+        for c in range(SIDE):
+            tanh(1, c)
+        gate(1, 0)
+        store(0, 0, 1, 0, N)
+        quantize(w_codes[1], w_scales[1], w_bf[1])
+        quantize(u_codes[1], u_scales[1], u_bf[1])
+        gate(1, 1)
+        store(0, 1, 2, 0, N)
+        s_il(x_bf[2], x_raw[2], 128, W)
+        v_il(x_bf[2], x_raw[2], 0, 128)
+        gate(1, 2)
+        store(0, 2, 3, 0, N)
+        quantize(x_codes[2], x_scales[2], x_bf[2])
+        gate(1, 3)
+        store(0, 3, 4, 0, N)
+        products(2)
+        s_il(x_bf[3], x_raw[3], 160, W)
+        v_il(x_bf[3], x_raw[3], 0, 160)
+        for c in range(SIDE):
+            tanh(2, c)
+        gate(2, 0)
+        quantize(x_codes[3], x_scales[3], x_bf[3])
+        gate(2, 1)
+        store(1, 0, 2, 0, W)
+        gate(2, 2)
+        gate(2, 3)
+        store(1, 2, 4, 0, W)
+        products(3)
+        for c in range(SIDE):
+            tanh(3, c)
+        for c in range(SIDE):
+            gate(3, c)
+            store(1, c, c + 1, W, N)

@@ -10,178 +10,137 @@ BF16 = mybir.dt.bfloat16
 U32 = mybir.dt.uint32
 U8 = mybir.dt.uint8
 FP8X4 = mybir.dt.float8_e4m3fn_x4
-ACT = mybir.ActivationFunctionType
-ALU = mybir.AluOpType
 
 P = 128
 PACK = 4
-ROWS = 32
-SIDE = 4
+TILE_ROWS = D // PACK
+SIDE = P // TILE_ROWS
 SETS = G // SIDE
-NMM = 128
-W = 256
+BLOCK = 32
 RUN = 4
-
-
-def interleave(copy, dst, src, lo, hi):
-    copy(
-        out=dst[:, lo:hi, :].rearrange("p (c i) t -> p c t i", i=RUN),
-        in_=src[:, :, lo:hi].rearrange("p t (c i) -> p c t i", i=RUN),
-    )
+HALF = N // 2
+X_ON_VECTOR = 160
+W_ON_VECTOR = 64
 
 
 def tile_rows_gglu_tanh_bias_kernel(tc, x, w, u, b, out):
     nc = tc.nc
-    x_rows = x.rearrange("g d n -> (g d) n")
-    w_rows = w.rearrange("g d m -> (g d) m")
-    u_rows = u.rearrange("g d m -> (g d) m")
-    b_rows = b.rearrange("g m o -> g (m o)")
-    chunks = [(s, n0) for s in range(SETS) for n0 in range(0, N, W)]
-
-    def set_rows(rows, s):
-        return rows[s * P * PACK : (s + 1) * P * PACK, :].rearrange("(p j) n -> p j n", j=PACK)
 
     with ExitStack() as ctx:
-        sb = ctx.enter_context(tc.tile_pool(name="sb", bufs=1))
-        ps = ctx.enter_context(tc.psum_pool(name="ps", bufs=1))
+        sbuf = ctx.enter_context(tc.tile_pool(name="sbuf", bufs=1))
+        psum = ctx.enter_context(tc.psum_pool(name="psum", bufs=1))
         ctx.enter_context(tc.manual_schedule())
 
-        def tiles(name, count, shape, dtype):
-            return [sb.tile(shape, dtype, name="%s%d" % (name, i), align_bytes=64) for i in range(count)]
+        def operand(name, source, s):
+            width = source.shape[2]
+            rows = source.rearrange("g d n -> (g d) n")[s * SIDE * D : (s + 1) * SIDE * D, :]
+            return {
+                "hbm": rows.rearrange("(p j) n -> p j n", j=PACK),
+                "raw": sbuf.tile([P, PACK, width], F32, name=name + "_raw", align_bytes=64),
+                "grouped": sbuf.tile([P, width, PACK], BF16, name=name + "_grouped", align_bytes=64),
+                "codes": sbuf.tile([P, width], U32, name=name + "_codes", align_bytes=64),
+                "scales": sbuf.tile([P, width], U8, name=name + "_scales", align_bytes=64),
+            }
 
-        w_raw = tiles("w_raw", SETS, [P, PACK, M], F32)
-        u_raw = tiles("u_raw", SETS, [P, PACK, M], F32)
-        w_bf = tiles("w_bf", SETS, [P, M, PACK], BF16)
-        u_bf = tiles("u_bf", SETS, [P, M, PACK], BF16)
-        w_codes = tiles("w_codes", SETS, [P, M], U32)
-        u_codes = tiles("u_codes", SETS, [P, M], U32)
-        w_scales = tiles("w_scales", SETS, [P, M], U8)
-        u_scales = tiles("u_scales", SETS, [P, M], U8)
-        x_raw = tiles("x_raw", len(chunks), [P, PACK, W], F32)
-        x_bf = tiles("x_bf", len(chunks), [P, W, PACK], BF16)
-        x_codes = tiles("x_codes", len(chunks), [P, W], U32)
-        x_scales = tiles("x_scales", len(chunks), [P, W], U8)
-        act = tiles("act", G, [P, N], F32)
-        y = tiles("y", SETS, [P, SIDE, N], F32)
-        b_stage = sb.tile([P, ROWS], F32, name="b_stage", align_bytes=64)
-        b_cols = sb.tile([P, ROWS], F32, name="b_cols", align_bytes=64)
-        h_bank = [ps.tile([P, N], F32, name="h_bank%d" % c) for c in range(SIDE)]
-        g_bank = [ps.tile([P, N], F32, name="g_bank%d" % c) for c in range(SIDE)]
+        xs = [operand("x%d" % s, x, s) for s in range(SETS)]
+        ws = [operand("w%d" % s, w, s) for s in range(SETS)]
+        us = [operand("u%d" % s, u, s) for s in range(SETS)]
+        activated = [sbuf.tile([P, N], F32, name="activated%d" % g, align_bytes=64) for g in range(G)]
+        result = [sbuf.tile([P, N], F32, name="result%d" % g, align_bytes=64) for g in range(G)]
+        bias_rows = sbuf.tile([P, BLOCK], F32, name="bias_rows", align_bytes=64)
+        bias_cols = sbuf.tile([P, BLOCK], F32, name="bias_cols", align_bytes=64)
+        w_bank = [psum.tile([M, N], F32, name="w_bank%d" % c) for c in range(SIDE)]
+        u_bank = [psum.tile([M, N], F32, name="u_bank%d" % c) for c in range(SIDE)]
 
-        def load_x(k):
-            s, n0 = chunks[k]
-            nc.sync.dma_start(out=x_raw[k][:], in_=set_rows(x_rows, s)[:, :, n0 : n0 + W])
+        def load(op):
+            nc.sync.dma_start(out=op["raw"][:], in_=op["hbm"])
 
-        def load_wu(s):
-            nc.sync.dma_start(out=w_raw[s][:], in_=set_rows(w_rows, s))
-            nc.sync.dma_start(out=u_raw[s][:], in_=set_rows(u_rows, s))
+        def interleave(copy, op, lo, hi):
+            copy(
+                out=op["grouped"][:, lo:hi, :].rearrange("p (c i) j -> p c j i", i=RUN),
+                in_=op["raw"][:, :, lo:hi].rearrange("p j (c i) -> p c j i", i=RUN),
+            )
 
-        def quantize(codes, scales, bf):
+        def interleave_shared(op, lo, hi, on_vector):
+            interleave(nc.vector.tensor_copy, op, lo, lo + on_vector)
+            interleave(nc.scalar.copy, op, lo + on_vector, hi)
+
+        def interleave_x(s):
+            for lo in range(0, N, HALF):
+                interleave_shared(xs[s], lo, lo + HALF, X_ON_VECTOR)
+
+        def quantize(op, lo, hi):
             nc.vector.quantize_mx(
-                out=codes[:].bitcast(FP8X4), scales=scales[:], in_=bf[:].rearrange("p n t -> p (n t)")
+                out=op["codes"][:, lo:hi].bitcast(FP8X4),
+                scales=op["scales"][:, lo:hi],
+                in_=op["grouped"][:, lo:hi, :].rearrange("p n j -> p (n j)"),
             )
 
-        def v_il(dst, src, lo, hi):
-            interleave(nc.vector.tensor_copy, dst, src, lo, hi)
+        def products(banks, weights, s):
+            for c in range(SIDE):
+                rows = slice(TILE_ROWS * c, TILE_ROWS * (c + 1))
+                nc.tensor.matmul_mx(
+                    out=banks[c][:],
+                    lhsT=weights["codes"][rows, :].bitcast(FP8X4),
+                    lhsT_scale=weights["scales"][rows, :],
+                    rhs=xs[s]["codes"][rows, :].bitcast(FP8X4),
+                    rhs_scale=xs[s]["scales"][rows, :],
+                    start=True,
+                    stop=True,
+                )
 
-        def s_il(dst, src, lo, hi):
-            interleave(nc.scalar.copy, dst, src, lo, hi)
-
-        def products(k):
-            s, n0 = chunks[k]
-            for banks, codes, scales in ((h_bank, w_codes, w_scales), (g_bank, u_codes, u_scales)):
-                for o in range(0, W, NMM):
-                    for c in range(SIDE):
-                        r = slice(ROWS * c, ROWS * (c + 1))
-                        nc.tensor.matmul_mx(
-                            out=banks[c][:, n0 + o : n0 + o + NMM],
-                            lhsT=codes[s][r, :].bitcast(FP8X4),
-                            lhsT_scale=scales[s][r, :],
-                            rhs=x_codes[k][r, o : o + NMM].bitcast(FP8X4),
-                            rhs_scale=x_scales[k][r, o : o + NMM],
-                            start=True,
-                            stop=True,
-                        )
-
-        def tanh(k, c):
-            s, n0 = chunks[k]
-            g = SIDE * s + c
+        def activate(g):
             nc.scalar.activation(
-                out=act[g][:, n0 : n0 + W], in_=h_bank[c][:, n0 : n0 + W], func=ACT.Tanh, bias=b_cols[:, g : g + 1]
+                out=activated[g][:],
+                in_=w_bank[g % SIDE][:],
+                func=mybir.ActivationFunctionType.Tanh,
+                bias=bias_cols[:, g : g + 1],
             )
 
-        def gate(k, c):
-            s, n0 = chunks[k]
-            g = SIDE * s + c
+        def gate_and_store(g):
             nc.vector.tensor_tensor(
-                out=y[s][:, c, n0 : n0 + W], in0=g_bank[c][:, n0 : n0 + W], in1=act[g][:, n0 : n0 + W], op=ALU.mult
+                out=result[g][:], in0=u_bank[g % SIDE][:], in1=activated[g][:], op=mybir.AluOpType.mult
             )
+            nc.sync.dma_start(out=out[g], in_=result[g][:])
 
-        def store(s, c0, c1, n0, n1):
-            g0 = SIDE * s
-            nc.sync.dma_start(
-                out=out[g0 + c0 : g0 + c1, :, n0:n1].rearrange("g m n -> m g n"), in_=y[s][:, c0:c1, n0:n1]
+        load(xs[0])
+        nc.gpsimd.memset(bias_rows[:], 0.0)
+        b_by_group = b.rearrange("g m o -> g (m o)")
+        for q in range(P // BLOCK):
+            nc.scalar.dma_start(
+                out=bias_rows[BLOCK * q : BLOCK * q + G, :], in_=b_by_group[:, BLOCK * q : BLOCK * (q + 1)]
             )
+        for op in (ws[0], us[0], ws[1], xs[1], us[1]):
+            load(op)
 
-        load_wu(0)
-        load_x(0)
-        load_x(1)
-        load_wu(1)
-        load_x(2)
-        load_x(3)
-        nc.gpsimd.memset(b_stage[:], 0.0)
-        for q in range(SIDE):
-            nc.gpsimd.dma_start(out=b_stage[ROWS * q : ROWS * q + G, :], in_=b_rows[:, ROWS * q : ROWS * (q + 1)])
+        interleave_x(0)
+        quantize(xs[0], 0, HALF)
+        interleave_shared(ws[0], 0, M, W_ON_VECTOR)
+        quantize(xs[0], HALF, N)
+        quantize(ws[0], 0, M)
+        products(w_bank, ws[0], 0)
+        interleave(nc.vector.tensor_copy, us[0], 0, M)
+        nc.vector.transpose(out=bias_cols[:], in_=bias_rows[:])
+        quantize(us[0], 0, M)
+        products(u_bank, us[0], 0)
+        interleave(nc.vector.tensor_copy, ws[1], 0, M)
+        quantize(ws[1], 0, M)
 
-        v_il(w_bf[0], w_raw[0], 0, M)
-        v_il(u_bf[0], u_raw[0], 0, M)
-        quantize(w_codes[0], w_scales[0], w_bf[0])
-        quantize(u_codes[0], u_scales[0], u_bf[0])
-        v_il(x_bf[0], x_raw[0], 0, W)
-        nc.vector.transpose(out=b_cols[:], in_=b_stage[:])
-        quantize(x_codes[0], x_scales[0], x_bf[0])
-        products(0)
-        v_il(x_bf[1], x_raw[1], 0, W)
-        for c in range(SIDE):
-            tanh(0, c)
-        gate(0, 0)
-        quantize(x_codes[1], x_scales[1], x_bf[1])
-        products(1)
-        s_il(w_bf[1], w_raw[1], 0, M)
-        gate(0, 1)
-        gate(0, 2)
-        gate(0, 3)
-        v_il(u_bf[1], u_raw[1], 0, M)
-        for c in range(SIDE):
-            tanh(1, c)
-        gate(1, 0)
-        store(0, 0, 1, 0, N)
-        quantize(w_codes[1], w_scales[1], w_bf[1])
-        quantize(u_codes[1], u_scales[1], u_bf[1])
-        gate(1, 1)
-        store(0, 1, 2, 0, N)
-        s_il(x_bf[2], x_raw[2], 128, W)
-        v_il(x_bf[2], x_raw[2], 0, 128)
-        gate(1, 2)
-        store(0, 2, 3, 0, N)
-        quantize(x_codes[2], x_scales[2], x_bf[2])
-        gate(1, 3)
-        store(0, 3, 4, 0, N)
-        products(2)
-        s_il(x_bf[3], x_raw[3], 160, W)
-        v_il(x_bf[3], x_raw[3], 0, 160)
-        for c in range(SIDE):
-            tanh(2, c)
-        gate(2, 0)
-        quantize(x_codes[3], x_scales[3], x_bf[3])
-        gate(2, 1)
-        store(1, 0, 2, 0, W)
-        gate(2, 2)
-        gate(2, 3)
-        store(1, 2, 4, 0, W)
-        products(3)
-        for c in range(SIDE):
-            tanh(3, c)
-        for c in range(SIDE):
-            gate(3, c)
-            store(1, c, c + 1, W, N)
+        for g in range(SIDE - 1):
+            activate(g)
+        for g in range(SIDE - 2):
+            gate_and_store(g)
+        interleave_x(1)
+        quantize(xs[1], 0, HALF)
+        quantize(xs[1], HALF, N)
+        interleave(nc.scalar.copy, us[1], 0, M)
+        activate(SIDE - 1)
+        products(w_bank, ws[1], 1)
+        gate_and_store(SIDE - 2)
+        quantize(us[1], 0, M)
+        gate_and_store(SIDE - 1)
+        products(u_bank, us[1], 1)
+
+        for g in range(SIDE, G):
+            activate(g)
+            gate_and_store(g)

@@ -19,8 +19,9 @@ SETS = G // SIDE
 BLOCK = 32
 RUN = 4
 HALF = N // 2
-X_ON_VECTOR = 160
-W_ON_VECTOR = 64
+QUARTER = N // 4
+BIAS_STEP = BLOCK // G
+X_ON_VECTOR = (384, 320)
 
 
 def tile_rows_gglu_tanh_bias_kernel(tc, x, w, u, b, out):
@@ -61,14 +62,6 @@ def tile_rows_gglu_tanh_bias_kernel(tc, x, w, u, b, out):
                 in_=op["raw"][:, :, lo:hi].rearrange("p j (c i) -> p c j i", i=RUN),
             )
 
-        def interleave_shared(op, lo, hi, on_vector):
-            interleave(nc.vector.tensor_copy, op, lo, lo + on_vector)
-            interleave(nc.scalar.copy, op, lo + on_vector, hi)
-
-        def interleave_x(s):
-            for lo in range(0, N, HALF):
-                interleave_shared(xs[s], lo, lo + HALF, X_ON_VECTOR)
-
         def quantize(op, lo, hi):
             nc.vector.quantize_mx(
                 out=op["codes"][:, lo:hi].bitcast(FP8X4),
@@ -76,71 +69,96 @@ def tile_rows_gglu_tanh_bias_kernel(tc, x, w, u, b, out):
                 in_=op["grouped"][:, lo:hi, :].rearrange("p n j -> p (n j)"),
             )
 
-        def products(banks, weights, s):
-            for c in range(SIDE):
-                rows = slice(TILE_ROWS * c, TILE_ROWS * (c + 1))
-                nc.tensor.matmul_mx(
-                    out=banks[c][:],
-                    lhsT=weights["codes"][rows, :].bitcast(FP8X4),
-                    lhsT_scale=weights["scales"][rows, :],
-                    rhs=xs[s]["codes"][rows, :].bitcast(FP8X4),
-                    rhs_scale=xs[s]["scales"][rows, :],
-                    start=True,
-                    stop=True,
-                )
+        def product(banks, weights, g):
+            s, c = divmod(g, SIDE)
+            rows = slice(TILE_ROWS * c, TILE_ROWS * (c + 1))
+            nc.tensor.matmul_mx(
+                out=banks[c][:],
+                lhsT=weights[s]["codes"][rows, :].bitcast(FP8X4),
+                lhsT_scale=weights[s]["scales"][rows, :],
+                rhs=xs[s]["codes"][rows, :].bitcast(FP8X4),
+                rhs_scale=xs[s]["scales"][rows, :],
+                start=True,
+                stop=True,
+            )
 
-        def activate(g):
+        def activate(g, lo=0, hi=N):
             nc.scalar.activation(
-                out=activated[g][:],
-                in_=w_bank[g % SIDE][:],
+                out=activated[g][:, lo:hi],
+                in_=w_bank[g % SIDE][:, lo:hi],
                 func=mybir.ActivationFunctionType.Tanh,
-                bias=bias_cols[:, g : g + 1],
+                bias=bias_cols[:, BIAS_STEP * g : BIAS_STEP * g + 1],
             )
 
-        def gate_and_store(g):
+        def gate(g, lo=0, hi=N):
             nc.vector.tensor_tensor(
-                out=result[g][:], in0=u_bank[g % SIDE][:], in1=activated[g][:], op=mybir.AluOpType.mult
+                out=result[g][:, lo:hi],
+                in0=u_bank[g % SIDE][:, lo:hi],
+                in1=activated[g][:, lo:hi],
+                op=mybir.AluOpType.mult,
             )
-            nc.sync.dma_start(out=out[g], in_=result[g][:])
+
+        def store(g, lo=0, hi=N):
+            nc.sync.dma_start(out=out[g][:, lo:hi], in_=result[g][:, lo:hi])
+
+        def in_halves(step, g):
+            step(g, 0, HALF)
+            step(g, HALF, N)
 
         load(xs[0])
-        nc.gpsimd.memset(bias_rows[:], 0.0)
-        b_by_group = b.rearrange("g m o -> g (m o)")
-        for q in range(P // BLOCK):
-            nc.scalar.dma_start(
-                out=bias_rows[BLOCK * q : BLOCK * q + G, :], in_=b_by_group[:, BLOCK * q : BLOCK * (q + 1)]
-            )
+        nc.vector.memset(bias_rows[:], 0.0)
+        nc.scalar.dma_start(out=bias_rows[0:P:BIAS_STEP, :], in_=b.rearrange("g (q i) o -> q g (i o)", i=BLOCK))
         for op in (ws[0], us[0], ws[1], xs[1], us[1]):
             load(op)
 
-        interleave_x(0)
+        interleave(nc.vector.tensor_copy, xs[0], 0, HALF)
+        interleave(nc.scalar.copy, xs[0], X_ON_VECTOR[0], N)
+        interleave(nc.vector.tensor_copy, xs[0], HALF, X_ON_VECTOR[0])
+        interleave(nc.scalar.copy, ws[0], 0, M)
         quantize(xs[0], 0, HALF)
-        interleave_shared(ws[0], 0, M, W_ON_VECTOR)
         quantize(xs[0], HALF, N)
         quantize(ws[0], 0, M)
-        products(w_bank, ws[0], 0)
-        interleave(nc.vector.tensor_copy, us[0], 0, M)
+        for g in range(SIDE):
+            product(w_bank, ws, g)
+        interleave(nc.scalar.copy, us[0], 0, M)
         nc.vector.transpose(out=bias_cols[:], in_=bias_rows[:])
         quantize(us[0], 0, M)
-        products(u_bank, us[0], 0)
-        interleave(nc.vector.tensor_copy, ws[1], 0, M)
+        for g in range(SIDE):
+            product(u_bank, us, g)
+        interleave(nc.scalar.copy, ws[1], 0, M)
         quantize(ws[1], 0, M)
 
-        for g in range(SIDE - 1):
-            activate(g)
-        for g in range(SIDE - 2):
-            gate_and_store(g)
-        interleave_x(1)
-        quantize(xs[1], 0, HALF)
+        in_halves(activate, 0)
+        activate(1)
+        in_halves(gate, 0)
+        store(0)
+
+        interleave(nc.vector.tensor_copy, xs[1], 0, QUARTER)
+        interleave(nc.scalar.copy, xs[1], X_ON_VECTOR[1], N)
+        interleave(nc.vector.tensor_copy, xs[1], QUARTER, X_ON_VECTOR[1])
+        quantize(xs[1], 0, QUARTER)
+        quantize(xs[1], QUARTER, HALF)
         quantize(xs[1], HALF, N)
         interleave(nc.scalar.copy, us[1], 0, M)
-        activate(SIDE - 1)
-        products(w_bank, ws[1], 1)
-        gate_and_store(SIDE - 2)
+        product(w_bank, ws, 4)
+        product(w_bank, ws, 5)
+        gate(1)
+        store(1)
+        activate(2)
         quantize(us[1], 0, M)
-        gate_and_store(SIDE - 1)
-        products(u_bank, us[1], 1)
+        product(w_bank, ws, 6)
+        product(u_bank, us, 4)
+        product(u_bank, us, 5)
+        gate(2)
+        store(2)
+        activate(3)
+        product(w_bank, ws, 7)
+        product(u_bank, us, 6)
+        gate(3)
+        store(3)
+        product(u_bank, us, 7)
 
         for g in range(SIDE, G):
-            activate(g)
-            gate_and_store(g)
+            in_halves(activate, g)
+            in_halves(gate, g)
+            store(g)

@@ -118,13 +118,17 @@ def tile_rows_gglu_tanh_bias_kernel(tc, x, w, u, b, out):
         quantize(xs[0], 0, HALF)
         quantize(xs[0], HALF, N)
         quantize(ws[0], 0, M)
-        for g in range(SIDE):
-            product(w_bank, ws, g)
+        product(w_bank, ws, 0)
+        product(w_bank, ws, 1)
         interleave(nc.scalar.copy, us[0], 0, M)
         nc.vector.transpose(out=bias_cols[:], in_=bias_rows[:])
         quantize(us[0], 0, M)
-        for g in range(SIDE):
-            product(u_bank, us, g)
+        product(u_bank, us, 0)
+        product(w_bank, ws, 2)
+        product(u_bank, us, 1)
+        product(w_bank, ws, 3)
+        product(u_bank, us, 2)
+        product(u_bank, us, 3)
         interleave(nc.scalar.copy, ws[1], 0, M)
         quantize(ws[1], 0, M)
 

@@ -21,7 +21,7 @@ RUN = 4
 HALF = N // 2
 QUARTER = N // 4
 BIAS_STEP = BLOCK // G
-X_ON_VECTOR = (384, 320)
+X_ON_VECTOR = (384, 416)
 
 
 def tile_rows_gglu_tanh_bias_kernel(tc, x, w, u, b, out):
@@ -32,18 +32,22 @@ def tile_rows_gglu_tanh_bias_kernel(tc, x, w, u, b, out):
         psum = ctx.enter_context(tc.psum_pool(name="psum", bufs=1))
         ctx.enter_context(tc.manual_schedule())
 
-        def operand(name, source, s):
+        def operand(name, source, s, loads=1):
             width = source.shape[2]
+            part = width // loads
             rows = source.rearrange("g d n -> (g d) n")[s * SIDE * D : (s + 1) * SIDE * D, :]
             return {
                 "hbm": rows.rearrange("(p j) n -> p j n", j=PACK),
-                "raw": sbuf.tile([P, PACK, width], F32, name=name + "_raw", align_bytes=64),
+                "part": part,
+                "raw": [
+                    sbuf.tile([P, PACK, part], F32, name="%s_raw%d" % (name, k), align_bytes=64) for k in range(loads)
+                ],
                 "grouped": sbuf.tile([P, width, PACK], BF16, name=name + "_grouped", align_bytes=64),
                 "codes": sbuf.tile([P, width], U32, name=name + "_codes", align_bytes=64),
                 "scales": sbuf.tile([P, width], U8, name=name + "_scales", align_bytes=64),
             }
 
-        xs = [operand("x%d" % s, x, s) for s in range(SETS)]
+        xs = [operand("x0", x, 0), operand("x1", x, 1, loads=2)]
         ws = [operand("w%d" % s, w, s) for s in range(SETS)]
         us = [operand("u%d" % s, u, s) for s in range(SETS)]
         activated = [sbuf.tile([P, N], F32, name="activated%d" % g, align_bytes=64) for g in range(G)]
@@ -54,12 +58,14 @@ def tile_rows_gglu_tanh_bias_kernel(tc, x, w, u, b, out):
         u_bank = [psum.tile([M, N], F32, name="u_bank%d" % c) for c in range(SIDE)]
 
         def load(op):
-            nc.sync.dma_start(out=op["raw"][:], in_=op["hbm"])
+            for k, raw in enumerate(op["raw"]):
+                nc.sync.dma_start(out=raw[:], in_=op["hbm"][:, :, k * op["part"] : (k + 1) * op["part"]])
 
         def interleave(copy, op, lo, hi):
+            k, first = divmod(lo, op["part"])
             copy(
                 out=op["grouped"][:, lo:hi, :].rearrange("p (c i) j -> p c j i", i=RUN),
-                in_=op["raw"][:, :, lo:hi].rearrange("p j (c i) -> p c j i", i=RUN),
+                in_=op["raw"][k][:, :, first : first + hi - lo].rearrange("p j (c i) -> p c j i", i=RUN),
             )
 
         def quantize(op, lo, hi):
@@ -132,22 +138,21 @@ def tile_rows_gglu_tanh_bias_kernel(tc, x, w, u, b, out):
         interleave(nc.scalar.copy, ws[1], 0, M)
         quantize(ws[1], 0, M)
 
+        interleave(nc.vector.tensor_copy, xs[1], 0, HALF)
         in_halves(activate, 0)
         activate(1)
-        in_halves(gate, 0)
-        store(0)
-
-        interleave(nc.vector.tensor_copy, xs[1], 0, QUARTER)
+        gate(0, 0, HALF)
+        quantize(xs[1], 0, HALF)
+        interleave(nc.vector.tensor_copy, xs[1], HALF, X_ON_VECTOR[1])
         interleave(nc.scalar.copy, xs[1], X_ON_VECTOR[1], N)
-        interleave(nc.vector.tensor_copy, xs[1], QUARTER, X_ON_VECTOR[1])
-        quantize(xs[1], 0, QUARTER)
-        quantize(xs[1], QUARTER, HALF)
+        gate(0, HALF, N)
+        store(0)
         quantize(xs[1], HALF, N)
+        gate(1)
+        store(1)
         interleave(nc.scalar.copy, us[1], 0, M)
         product(w_bank, ws, 4)
         product(w_bank, ws, 5)
-        gate(1)
-        store(1)
         activate(2)
         quantize(us[1], 0, M)
         product(w_bank, ws, 6)

@@ -19,9 +19,9 @@ SETS = G // SIDE
 BLOCK = 32
 RUN = 4
 HALF = N // 2
-QUARTER = N // 4
 BIAS_STEP = BLOCK // G
-X_ON_VECTOR = (384, 416)
+X0_ON_VECTOR = 384
+X1_ON_VECTOR = (192, 160)
 
 
 def tile_rows_gglu_tanh_bias_kernel(tc, x, w, u, b, out):
@@ -57,9 +57,8 @@ def tile_rows_gglu_tanh_bias_kernel(tc, x, w, u, b, out):
         w_bank = [psum.tile([M, N], F32, name="w_bank%d" % c) for c in range(SIDE)]
         u_bank = [psum.tile([M, N], F32, name="u_bank%d" % c) for c in range(SIDE)]
 
-        def load(op):
-            for k, raw in enumerate(op["raw"]):
-                nc.sync.dma_start(out=raw[:], in_=op["hbm"][:, :, k * op["part"] : (k + 1) * op["part"]])
+        def load(op, k=0):
+            nc.sync.dma_start(out=op["raw"][k][:], in_=op["hbm"][:, :, k * op["part"] : (k + 1) * op["part"]])
 
         def interleave(copy, op, lo, hi):
             k, first = divmod(lo, op["part"])
@@ -114,12 +113,16 @@ def tile_rows_gglu_tanh_bias_kernel(tc, x, w, u, b, out):
         load(xs[0])
         nc.vector.memset(bias_rows[:], 0.0)
         nc.scalar.dma_start(out=bias_rows[0:P:BIAS_STEP, :], in_=b.rearrange("g (q i) o -> q g (i o)", i=BLOCK))
-        for op in (ws[0], us[0], ws[1], xs[1], us[1]):
-            load(op)
+        load(ws[0])
+        load(us[0])
+        load(xs[1], 0)
+        load(ws[1])
+        load(xs[1], 1)
+        load(us[1])
 
         interleave(nc.vector.tensor_copy, xs[0], 0, HALF)
-        interleave(nc.scalar.copy, xs[0], X_ON_VECTOR[0], N)
-        interleave(nc.vector.tensor_copy, xs[0], HALF, X_ON_VECTOR[0])
+        interleave(nc.scalar.copy, xs[0], X0_ON_VECTOR, N)
+        interleave(nc.vector.tensor_copy, xs[0], HALF, X0_ON_VECTOR)
         interleave(nc.scalar.copy, ws[0], 0, M)
         quantize(xs[0], 0, HALF)
         quantize(xs[0], HALF, N)
@@ -135,25 +138,28 @@ def tile_rows_gglu_tanh_bias_kernel(tc, x, w, u, b, out):
         product(w_bank, ws, 3)
         product(u_bank, us, 2)
         product(u_bank, us, 3)
-        interleave(nc.scalar.copy, ws[1], 0, M)
-        quantize(ws[1], 0, M)
 
-        interleave(nc.vector.tensor_copy, xs[1], 0, HALF)
+        interleave(nc.vector.tensor_copy, xs[1], 0, X1_ON_VECTOR[0])
+        interleave(nc.scalar.copy, xs[1], X1_ON_VECTOR[0], HALF)
         in_halves(activate, 0)
         activate(1)
-        gate(0, 0, HALF)
+        interleave(nc.vector.tensor_copy, ws[1], 0, M)
         quantize(xs[1], 0, HALF)
-        interleave(nc.vector.tensor_copy, xs[1], HALF, X_ON_VECTOR[1])
-        interleave(nc.scalar.copy, xs[1], X_ON_VECTOR[1], N)
+        gate(0, 0, HALF)
+        quantize(ws[1], 0, M)
         gate(0, HALF, N)
         store(0)
+        activate(2, 0, HALF)
+        interleave(nc.vector.tensor_copy, xs[1], HALF, HALF + X1_ON_VECTOR[1])
+        interleave(nc.scalar.copy, xs[1], HALF + X1_ON_VECTOR[1], N)
+        gate(1, 0, HALF)
         quantize(xs[1], HALF, N)
-        gate(1)
+        gate(1, HALF, N)
         store(1)
         interleave(nc.scalar.copy, us[1], 0, M)
         product(w_bank, ws, 4)
         product(w_bank, ws, 5)
-        activate(2)
+        activate(2, HALF, N)
         quantize(us[1], 0, M)
         product(w_bank, ws, 6)
         product(u_bank, us, 4)

@@ -17,11 +17,12 @@ TILE_ROWS = D // PACK
 SIDE = P // TILE_ROWS
 SETS = G // SIDE
 BLOCK = 32
+BIAS_STEP = BLOCK // G
 RUN = 4
 HALF = N // 2
-BIAS_STEP = BLOCK // G
 X0_ON_VECTOR = 384
-X1_ON_VECTOR = (192, 160)
+X1_FIRST_ON_VECTOR = 192
+X1_LAST_ON_VECTOR = 160
 
 
 def tile_rows_gglu_tanh_bias_kernel(tc, x, w, u, b, out):
@@ -67,6 +68,10 @@ def tile_rows_gglu_tanh_bias_kernel(tc, x, w, u, b, out):
                 in_=op["raw"][k][:, :, first : first + hi - lo].rearrange("p j (c i) -> p c j i", i=RUN),
             )
 
+        def interleave_shared(op, lo, hi, on_vector):
+            interleave(nc.vector.tensor_copy, op, lo, lo + on_vector)
+            interleave(nc.scalar.copy, op, lo + on_vector, hi)
+
         def quantize(op, lo, hi):
             nc.vector.quantize_mx(
                 out=op["codes"][:, lo:hi].bitcast(FP8X4),
@@ -87,6 +92,12 @@ def tile_rows_gglu_tanh_bias_kernel(tc, x, w, u, b, out):
                 stop=True,
             )
 
+        def w_product(g):
+            product(w_bank, ws, g)
+
+        def u_product(g):
+            product(u_bank, us, g)
+
         def activate(g, lo=0, hi=N):
             nc.scalar.activation(
                 out=activated[g][:, lo:hi],
@@ -103,8 +114,8 @@ def tile_rows_gglu_tanh_bias_kernel(tc, x, w, u, b, out):
                 op=mybir.AluOpType.mult,
             )
 
-        def store(g, lo=0, hi=N):
-            nc.sync.dma_start(out=out[g][:, lo:hi], in_=result[g][:, lo:hi])
+        def store(g):
+            nc.sync.dma_start(out=out[g], in_=result[g][:])
 
         def in_halves(step, g):
             step(g, 0, HALF)
@@ -112,35 +123,31 @@ def tile_rows_gglu_tanh_bias_kernel(tc, x, w, u, b, out):
 
         load(xs[0])
         nc.vector.memset(bias_rows[:], 0.0)
-        nc.scalar.dma_start(out=bias_rows[0:P:BIAS_STEP, :], in_=b.rearrange("g (q i) o -> q g (i o)", i=BLOCK))
         load(ws[0])
         load(us[0])
+        nc.sync.dma_start(out=bias_rows[0:P:BIAS_STEP, :], in_=b.rearrange("g (q i) o -> q g (i o)", i=BLOCK))
         load(xs[1], 0)
         load(ws[1])
         load(xs[1], 1)
         load(us[1])
 
         interleave(nc.vector.tensor_copy, xs[0], 0, HALF)
-        interleave(nc.scalar.copy, xs[0], X0_ON_VECTOR, N)
-        interleave(nc.vector.tensor_copy, xs[0], HALF, X0_ON_VECTOR)
+        interleave_shared(xs[0], HALF, N, X0_ON_VECTOR - HALF)
         interleave(nc.scalar.copy, ws[0], 0, M)
         quantize(xs[0], 0, HALF)
         quantize(xs[0], HALF, N)
         quantize(ws[0], 0, M)
-        product(w_bank, ws, 0)
-        product(w_bank, ws, 1)
+        w_product(0)
+        w_product(1)
         interleave(nc.scalar.copy, us[0], 0, M)
         nc.vector.transpose(out=bias_cols[:], in_=bias_rows[:])
         quantize(us[0], 0, M)
-        product(u_bank, us, 0)
-        product(w_bank, ws, 2)
-        product(u_bank, us, 1)
-        product(w_bank, ws, 3)
-        product(u_bank, us, 2)
-        product(u_bank, us, 3)
+        for g in range(SIDE):
+            u_product(g)
+            if g + 2 < SIDE:
+                w_product(g + 2)
 
-        interleave(nc.vector.tensor_copy, xs[1], 0, X1_ON_VECTOR[0])
-        interleave(nc.scalar.copy, xs[1], X1_ON_VECTOR[0], HALF)
+        interleave_shared(xs[1], 0, HALF, X1_FIRST_ON_VECTOR)
         in_halves(activate, 0)
         activate(1)
         interleave(nc.vector.tensor_copy, ws[1], 0, M)
@@ -149,29 +156,30 @@ def tile_rows_gglu_tanh_bias_kernel(tc, x, w, u, b, out):
         quantize(ws[1], 0, M)
         gate(0, HALF, N)
         store(0)
+
         activate(2, 0, HALF)
-        interleave(nc.vector.tensor_copy, xs[1], HALF, HALF + X1_ON_VECTOR[1])
-        interleave(nc.scalar.copy, xs[1], HALF + X1_ON_VECTOR[1], N)
+        interleave_shared(xs[1], HALF, N, X1_LAST_ON_VECTOR)
         gate(1, 0, HALF)
         quantize(xs[1], HALF, N)
         gate(1, HALF, N)
         store(1)
         interleave(nc.scalar.copy, us[1], 0, M)
-        product(w_bank, ws, 4)
-        product(w_bank, ws, 5)
+
+        w_product(SIDE)
+        w_product(SIDE + 1)
         activate(2, HALF, N)
         quantize(us[1], 0, M)
-        product(w_bank, ws, 6)
-        product(u_bank, us, 4)
-        product(u_bank, us, 5)
+        w_product(SIDE + 2)
+        u_product(SIDE)
+        u_product(SIDE + 1)
         gate(2)
         store(2)
         activate(3)
-        product(w_bank, ws, 7)
-        product(u_bank, us, 6)
+        w_product(SIDE + 3)
+        u_product(SIDE + 2)
         gate(3)
         store(3)
-        product(u_bank, us, 7)
+        u_product(SIDE + 3)
 
         for g in range(SIDE, G):
             in_halves(activate, g)

@@ -18,7 +18,7 @@ SIDE = P // TILE_ROWS
 SETS = G // SIDE
 BLOCK = 32
 BIAS_STEP = BLOCK // G
-RUN = 4
+RUN = 2
 HALF = N // 2
 X0_ON_VECTOR = 384
 X1_FIRST_ON_VECTOR = 192

@@ -20,6 +20,7 @@ BLOCK = 32
 BIAS_STEP = BLOCK // G
 RUN = 2
 HALF = N // 2
+ALIGN = 256
 X0_ON_VECTOR = 384
 X1_FIRST_ON_VECTOR = 192
 X1_LAST_ON_VECTOR = 160
@@ -41,20 +42,20 @@ def tile_rows_gglu_tanh_bias_kernel(tc, x, w, u, b, out):
                 "hbm": rows.rearrange("(p j) n -> p j n", j=PACK),
                 "part": part,
                 "raw": [
-                    sbuf.tile([P, PACK, part], F32, name="%s_raw%d" % (name, k), align_bytes=64) for k in range(loads)
+                    sbuf.tile([P, PACK, part], F32, name="%s_raw%d" % (name, k), align_bytes=ALIGN) for k in range(loads)
                 ],
-                "grouped": sbuf.tile([P, width, PACK], BF16, name=name + "_grouped", align_bytes=64),
-                "codes": sbuf.tile([P, width], U32, name=name + "_codes", align_bytes=64),
-                "scales": sbuf.tile([P, width], U8, name=name + "_scales", align_bytes=64),
+                "grouped": sbuf.tile([P, width, PACK], BF16, name=name + "_grouped", align_bytes=ALIGN),
+                "codes": sbuf.tile([P, width], U32, name=name + "_codes", align_bytes=ALIGN),
+                "scales": sbuf.tile([P, width], U8, name=name + "_scales", align_bytes=ALIGN),
             }
 
         xs = [operand("x0", x, 0), operand("x1", x, 1, loads=2)]
         ws = [operand("w%d" % s, w, s) for s in range(SETS)]
         us = [operand("u%d" % s, u, s) for s in range(SETS)]
-        activated = [sbuf.tile([P, N], F32, name="activated%d" % g, align_bytes=64) for g in range(G)]
-        result = [sbuf.tile([P, N], F32, name="result%d" % g, align_bytes=64) for g in range(G)]
-        bias_rows = sbuf.tile([P, BLOCK], F32, name="bias_rows", align_bytes=64)
-        bias_cols = sbuf.tile([P, BLOCK], F32, name="bias_cols", align_bytes=64)
+        activated = [sbuf.tile([P, N], F32, name="activated%d" % g, align_bytes=ALIGN) for g in range(G)]
+        result = [sbuf.tile([P, N], F32, name="result%d" % g, align_bytes=ALIGN) for g in range(G)]
+        bias_rows = sbuf.tile([P, BLOCK], F32, name="bias_rows", align_bytes=ALIGN)
+        bias_cols = sbuf.tile([P, BLOCK], F32, name="bias_cols", align_bytes=ALIGN)
         w_bank = [psum.tile([M, N], F32, name="w_bank%d" % c) for c in range(SIDE)]
         u_bank = [psum.tile([M, N], F32, name="u_bank%d" % c) for c in range(SIDE)]
 

@@ -22,8 +22,8 @@ RUN = 2
 HALF = N // 2
 ALIGN = 256
 X0_ON_VECTOR = 384
-X1_FIRST_ON_VECTOR = 192
-X1_LAST_ON_VECTOR = 160
+X1_FIRST_ON_VECTOR = 128
+X1_LAST_ON_VECTOR = 192
 
 
 def tile_rows_gglu_tanh_bias_kernel(tc, x, w, u, b, out):
@@ -153,36 +153,31 @@ def tile_rows_gglu_tanh_bias_kernel(tc, x, w, u, b, out):
         activate(1)
         interleave(nc.vector.tensor_copy, ws[1], 0, M)
         quantize(xs[1], 0, HALF)
-        gate(0, 0, HALF)
         quantize(ws[1], 0, M)
+        gate(0, 0, HALF)
+        interleave_shared(xs[1], HALF, N, X1_LAST_ON_VECTOR)
         gate(0, HALF, N)
         store(0)
-
-        activate(2, 0, HALF)
-        interleave_shared(xs[1], HALF, N, X1_LAST_ON_VECTOR)
-        gate(1, 0, HALF)
         quantize(xs[1], HALF, N)
-        gate(1, HALF, N)
-        store(1)
-        interleave(nc.scalar.copy, us[1], 0, M)
 
-        w_product(SIDE)
-        w_product(SIDE + 1)
-        activate(2, HALF, N)
+        w_product(4)
+        w_product(5)
+        interleave(nc.scalar.copy, us[1], 0, M)
+        gate(1)
+        store(1)
         quantize(us[1], 0, M)
-        w_product(SIDE + 2)
-        u_product(SIDE)
-        u_product(SIDE + 1)
-        gate(2)
-        store(2)
+        activate(2)
+        w_product(6)
+        u_product(4)
         activate(3)
-        w_product(SIDE + 3)
-        u_product(SIDE + 2)
-        gate(3)
-        store(3)
-        u_product(SIDE + 3)
+        w_product(7)
+        u_product(5)
+        for g in range(2, SIDE):
+            gate(g)
+            store(g)
+            u_product(g + SIDE)
 
         for g in range(SIDE, G):
-            in_halves(activate, g)
-            in_halves(gate, g)
+            activate(g)
+            gate(g)
             store(g)

from contextlib import ExitStack

import concourse.mybir as mybir

G, D, M, N = 8, 128, 128, 512
FLOPS = 2 * 2 * G * D * M * N

F32 = mybir.dt.float32
BF16 = mybir.dt.bfloat16
U32 = mybir.dt.uint32
U8 = mybir.dt.uint8
FP8X4 = mybir.dt.float8_e4m3fn_x4

P = 128
PACK = 4
TILE_ROWS = D // PACK
SIDE = P // TILE_ROWS
SETS = G // SIDE
BLOCK = 32
BIAS_STEP = BLOCK // G
RUN = 2
HALF = N // 2
ALIGN = 256
X0_ON_VECTOR = 384
X1_FIRST_ON_VECTOR = 128
X1_LAST_ON_VECTOR = 192


def tile_rows_gglu_tanh_bias_kernel(tc, x, w, u, b, out):
    nc = tc.nc

    with ExitStack() as ctx:
        sbuf = ctx.enter_context(tc.tile_pool(name="sbuf", bufs=1))
        psum = ctx.enter_context(tc.psum_pool(name="psum", bufs=1))
        ctx.enter_context(tc.manual_schedule())

        def operand(name, source, s, loads=1):
            width = source.shape[2]
            part = width // loads
            rows = source.rearrange("g d n -> (g d) n")[s * SIDE * D : (s + 1) * SIDE * D, :]
            return {
                "hbm": rows.rearrange("(p j) n -> p j n", j=PACK),
                "part": part,
                "raw": [
                    sbuf.tile([P, PACK, part], F32, name="%s_raw%d" % (name, k), align_bytes=ALIGN) for k in range(loads)
                ],
                "grouped": sbuf.tile([P, width, PACK], BF16, name=name + "_grouped", align_bytes=ALIGN),
                "codes": sbuf.tile([P, width], U32, name=name + "_codes", align_bytes=ALIGN),
                "scales": sbuf.tile([P, width], U8, name=name + "_scales", align_bytes=ALIGN),
            }

        xs = [operand("x0", x, 0), operand("x1", x, 1, loads=2)]
        ws = [operand("w%d" % s, w, s) for s in range(SETS)]
        us = [operand("u%d" % s, u, s) for s in range(SETS)]
        activated = [sbuf.tile([P, N], F32, name="activated%d" % g, align_bytes=ALIGN) for g in range(G)]
        result = [sbuf.tile([P, N], F32, name="result%d" % g, align_bytes=ALIGN) for g in range(G)]
        bias_rows = sbuf.tile([P, BLOCK], F32, name="bias_rows", align_bytes=ALIGN)
        bias_cols = sbuf.tile([P, BLOCK], F32, name="bias_cols", align_bytes=ALIGN)
        w_bank = [psum.tile([M, N], F32, name="w_bank%d" % c) for c in range(SIDE)]
        u_bank = [psum.tile([M, N], F32, name="u_bank%d" % c) for c in range(SIDE)]

        def load(op, k=0):
            nc.sync.dma_start(out=op["raw"][k][:], in_=op["hbm"][:, :, k * op["part"] : (k + 1) * op["part"]])

        def interleave(copy, op, lo, hi):
            k, first = divmod(lo, op["part"])
            copy(
                out=op["grouped"][:, lo:hi, :].rearrange("p (c i) j -> p c j i", i=RUN),
                in_=op["raw"][k][:, :, first : first + hi - lo].rearrange("p j (c i) -> p c j i", i=RUN),
            )

        def interleave_shared(op, lo, hi, on_vector):
            interleave(nc.vector.tensor_copy, op, lo, lo + on_vector)
            interleave(nc.scalar.copy, op, lo + on_vector, hi)

        def quantize(op, lo, hi):
            nc.vector.quantize_mx(
                out=op["codes"][:, lo:hi].bitcast(FP8X4),
                scales=op["scales"][:, lo:hi],
                in_=op["grouped"][:, lo:hi, :].rearrange("p n j -> p (n j)"),
            )

        def product(banks, weights, g):
            s, c = divmod(g, SIDE)
            rows = slice(TILE_ROWS * c, TILE_ROWS * (c + 1))
            nc.tensor.matmul_mx(
                out=banks[c][:],
                lhsT=weights[s]["codes"][rows, :].bitcast(FP8X4),
                lhsT_scale=weights[s]["scales"][rows, :],
                rhs=xs[s]["codes"][rows, :].bitcast(FP8X4),
                rhs_scale=xs[s]["scales"][rows, :],
                start=True,
                stop=True,
            )

        def w_product(g):
            product(w_bank, ws, g)

        def u_product(g):
            product(u_bank, us, g)

        def activate(g, lo=0, hi=N):
            nc.scalar.activation(
                out=activated[g][:, lo:hi],
                in_=w_bank[g % SIDE][:, lo:hi],
                func=mybir.ActivationFunctionType.Tanh,
                bias=bias_cols[:, BIAS_STEP * g : BIAS_STEP * g + 1],
            )

        def gate(g, lo=0, hi=N):
            nc.vector.tensor_tensor(
                out=result[g][:, lo:hi],
                in0=u_bank[g % SIDE][:, lo:hi],
                in1=activated[g][:, lo:hi],
                op=mybir.AluOpType.mult,
            )

        def store(g):
            nc.sync.dma_start(out=out[g], in_=result[g][:])

        def in_halves(step, g):
            step(g, 0, HALF)
            step(g, HALF, N)

        load(xs[0])
        nc.vector.memset(bias_rows[:], 0.0)
        load(ws[0])
        load(us[0])
        nc.sync.dma_start(out=bias_rows[0:P:BIAS_STEP, :], in_=b.rearrange("g (q i) o -> q g (i o)", i=BLOCK))
        load(xs[1], 0)
        load(ws[1])
        load(xs[1], 1)
        load(us[1])

        interleave(nc.vector.tensor_copy, xs[0], 0, HALF)
        interleave_shared(xs[0], HALF, N, X0_ON_VECTOR - HALF)
        interleave(nc.scalar.copy, ws[0], 0, M)
        quantize(xs[0], 0, HALF)
        quantize(xs[0], HALF, N)
        quantize(ws[0], 0, M)
        w_product(0)
        w_product(1)
        interleave(nc.scalar.copy, us[0], 0, M)
        nc.vector.transpose(out=bias_cols[:], in_=bias_rows[:])
        quantize(us[0], 0, M)
        for g in range(SIDE):
            u_product(g)
            if g + 2 < SIDE:
                w_product(g + 2)

        interleave_shared(xs[1], 0, HALF, X1_FIRST_ON_VECTOR)
        in_halves(activate, 0)
        activate(1)
        interleave(nc.vector.tensor_copy, ws[1], 0, M)
        quantize(xs[1], 0, HALF)
        quantize(ws[1], 0, M)
        gate(0, 0, HALF)
        interleave_shared(xs[1], HALF, N, X1_LAST_ON_VECTOR)
        gate(0, HALF, N)
        store(0)
        quantize(xs[1], HALF, N)

        w_product(4)
        w_product(5)
        interleave(nc.scalar.copy, us[1], 0, M)
        gate(1)
        store(1)
        quantize(us[1], 0, M)
        activate(2)
        w_product(6)
        u_product(4)
        activate(3)
        w_product(7)
        u_product(5)
        for g in range(2, SIDE):
            gate(g)
            store(g)
            u_product(g + SIDE)

        for g in range(SIDE, G):
            activate(g)
            gate(g)
            store(g)
